import numpy as np
CORES = [0,8]
N = 2
def setup_inputs(rng):
    return {"x": rng.standard_normal((N, 128, 16384), dtype=np.float32)}
def reference(x):
    s = x.sum(axis=0, dtype=np.float64).astype(x.dtype)
    return {"y": np.broadcast_to(s, (N,) + s.shape)}

@@ -1,0 +1,62 @@
+import concourse.bass as bass
+WIDTHS = [128, 384, 512, 512, 512, 512, 512, 512, 384, 128]
+NR = len(WIDTHS)
+STARTS = [4 * sum(WIDTHS[:r]) for r in range(NR)]
+HELP = (2, 3, 6, 7)
+PRE = 2
+LAG = 1
+SCRATCH = {'xs': ('sbuf', [128, 16384], 'float32'), 'land': ('sbuf', [128, 16384], 'float32')}
+SEMAPHORES = ['ld0', 'ld1', 'ld2', 'ld3', 'st', 'snt'] + ['a%d' % i for i in range(16)] + ['b%d' % i for i in range(16)]
+
+def rank_program(g, core, T, topo):
+    A = [T.sem.a0, T.sem.a1, T.sem.a2, T.sem.a3, T.sem.a4, T.sem.a5, T.sem.a6, T.sem.a7, T.sem.a8, T.sem.a9, T.sem.a10, T.sem.a11, T.sem.a12, T.sem.a13, T.sem.a14, T.sem.a15]
+    B = [T.sem.b0, T.sem.b1, T.sem.b2, T.sem.b3, T.sem.b4, T.sem.b5, T.sem.b6, T.sem.b7, T.sem.b8, T.sem.b9, T.sem.b10, T.sem.b11, T.sem.b12, T.sem.b13, T.sem.b14, T.sem.b15]
+    LD = [T.sem.ld0, T.sem.ld1, T.sem.ld2, T.sem.ld3]
+    base = topo.chip(core) * 8
+    root = base
+    on_chip = core - base
+
+    def rnd(t, r):
+        return t[:, STARTS[r]:STARTS[r] + 4 * WIDTHS[r]]
+
+    def blk(t, r, h):
+        c = STARTS[r] + h * WIDTHS[r]
+        return t[:, c:c + WIDTHS[r]]
+    if core == root:
+
+        def load(r):
+            g.dma_start(rnd(T.xs, r), rnd(T.x, r)).then_inc(LD[r % PRE], 16)
+        for r in range(min(PRE, NR)):
+            load(r)
+        for r in range(NR):
+            g.wait_ge(LD[r % PRE], 16 * (r // PRE + 1))
+            trs = []
+            for h in range(4):
+                rid, pid = topo.addr(base + HELP[h])[:2]
+                trs.append(bass.RemoteDMATransfer(dst_ids=[bass.DstId(rid=rid, pnc=pid)], dma_engine_mask=15 << 4 * h, remote_sem=A[r], src=blk(T.xs, r, h), dst=blk(T.xs, r, h)))
+            g.remote_dma_fused(trs, local_sem=T.sem.snt)
+            if r + PRE < NR:
+                load(r + PRE)
+        for r in range(NR):
+            g.wait_ge(A[r], 32)
+            g.dma_start(rnd(T.y, r), rnd(T.land, r)).then_inc(T.sem.st, 16)
+        g.wait_ge(T.sem.snt, 16 * NR)
+        g.wait_ge(T.sem.st, 16 * NR)
+        return
+    if on_chip not in HELP:
+        return
+    h = HELP.index(on_chip)
+    mate_rid, mate_pid = topo.addr(core ^ 8)[:2]
+    root_rid, root_pid = topo.addr(root)[:2]
+
+    def fold(r):
+        g.wait_ge(B[r], 8)
+        g.remote_dma_fused([bass.RemoteDMATransfer(dst_ids=[bass.DstId(rid=root_rid, pnc=root_pid)], dma_engine_mask=65280, remote_sem=A[r], srcs=[blk(T.xs, r, h), blk(T.land, r, h)], dsts=[blk(T.land, r, h)], alu_op=1)], local_sem=T.sem.snt)
+    for r in range(NR):
+        g.wait_ge(A[r], 4)
+        g.remote_dma(blk(T.land, r, h), blk(T.xs, r, h), B[r], T.sem.snt, mate_pid, mate_rid, 255)
+        if r >= LAG:
+            fold(r - LAG)
+    for r in range(NR - LAG, NR):
+        fold(r)
+    g.wait_ge(T.sem.snt, 16 * NR)

@@ -1,4 +1,5 @@
 import concourse.bass as bass
+
 WIDTHS = [128, 384, 512, 512, 512, 512, 512, 512, 384, 128]
 NR = len(WIDTHS)
 STARTS = [4 * sum(WIDTHS[:r]) for r in range(NR)]
@@ -6,12 +7,14 @@ HELP = (2, 3, 6, 7)
 PRE = 2
 LAG = 1
 SCRATCH = {'xs': ('sbuf', [128, 16384], 'float32'), 'land': ('sbuf', [128, 16384], 'float32')}
-SEMAPHORES = ['ld0', 'ld1', 'ld2', 'ld3', 'st', 'snt'] + ['a%d' % i for i in range(16)] + ['b%d' % i for i in range(16)]
+SEMAPHORES = (['st', 'snt'] + ['l%d' % i for i in range(16)]
+              + ['a%d' % i for i in range(16)] + ['b%d' % i for i in range(16)])
+
 
 def rank_program(g, core, T, topo):
     A = [T.sem.a0, T.sem.a1, T.sem.a2, T.sem.a3, T.sem.a4, T.sem.a5, T.sem.a6, T.sem.a7, T.sem.a8, T.sem.a9, T.sem.a10, T.sem.a11, T.sem.a12, T.sem.a13, T.sem.a14, T.sem.a15]
     B = [T.sem.b0, T.sem.b1, T.sem.b2, T.sem.b3, T.sem.b4, T.sem.b5, T.sem.b6, T.sem.b7, T.sem.b8, T.sem.b9, T.sem.b10, T.sem.b11, T.sem.b12, T.sem.b13, T.sem.b14, T.sem.b15]
-    LD = [T.sem.ld0, T.sem.ld1, T.sem.ld2, T.sem.ld3]
+    L = [T.sem.l0, T.sem.l1, T.sem.l2, T.sem.l3, T.sem.l4, T.sem.l5, T.sem.l6, T.sem.l7, T.sem.l8, T.sem.l9, T.sem.l10, T.sem.l11, T.sem.l12, T.sem.l13, T.sem.l14, T.sem.l15]
     base = topo.chip(core) * 8
     root = base
     on_chip = core - base
@@ -22,26 +25,26 @@ def rank_program(g, core, T, topo):
     def blk(t, r, h):
         c = STARTS[r] + h * WIDTHS[r]
         return t[:, c:c + WIDTHS[r]]
-    if core == root:
 
-        def load(r):
-            g.dma_start(rnd(T.xs, r), rnd(T.x, r)).then_inc(LD[r % PRE], 16)
-        for r in range(min(PRE, NR)):
-            load(r)
+    if core == root:
         for r in range(NR):
-            g.wait_ge(LD[r % PRE], 16 * (r // PRE + 1))
+            if r >= PRE:
+                g.sync.wait_ge(L[r - PRE], 16)
+            g.sync.dma_start(rnd(T.xs, r), rnd(T.x, r)).then_inc(L[r], 16)
+        for r in range(NR):
+            g.wait_ge(L[r], 16)
             trs = []
             for h in range(4):
                 rid, pid = topo.addr(base + HELP[h])[:2]
-                trs.append(bass.RemoteDMATransfer(dst_ids=[bass.DstId(rid=rid, pnc=pid)], dma_engine_mask=15 << 4 * h, remote_sem=A[r], src=blk(T.xs, r, h), dst=blk(T.xs, r, h)))
+                trs.append(bass.RemoteDMATransfer(
+                    dst_ids=[bass.DstId(rid=rid, pnc=pid)], dma_engine_mask=15 << 4 * h,
+                    remote_sem=A[r], src=blk(T.xs, r, h), dst=blk(T.xs, r, h)))
             g.remote_dma_fused(trs, local_sem=T.sem.snt)
-            if r + PRE < NR:
-                load(r + PRE)
         for r in range(NR):
-            g.wait_ge(A[r], 32)
-            g.dma_start(rnd(T.y, r), rnd(T.land, r)).then_inc(T.sem.st, 16)
+            g.scalar.wait_ge(A[r], 32)
+            g.scalar.dma_start(rnd(T.y, r), rnd(T.land, r)).then_inc(T.sem.st, 16)
         g.wait_ge(T.sem.snt, 16 * NR)
-        g.wait_ge(T.sem.st, 16 * NR)
+        g.scalar.wait_ge(T.sem.st, 16 * NR)
         return
     if on_chip not in HELP:
         return
@@ -51,7 +54,11 @@ def rank_program(g, core, T, topo):
 
     def fold(r):
         g.wait_ge(B[r], 8)
-        g.remote_dma_fused([bass.RemoteDMATransfer(dst_ids=[bass.DstId(rid=root_rid, pnc=root_pid)], dma_engine_mask=65280, remote_sem=A[r], srcs=[blk(T.xs, r, h), blk(T.land, r, h)], dsts=[blk(T.land, r, h)], alu_op=1)], local_sem=T.sem.snt)
+        g.remote_dma_fused([bass.RemoteDMATransfer(
+            dst_ids=[bass.DstId(rid=root_rid, pnc=root_pid)], dma_engine_mask=65280,
+            remote_sem=A[r], srcs=[blk(T.xs, r, h), blk(T.land, r, h)],
+            dsts=[blk(T.land, r, h)], alu_op=1)], local_sem=T.sem.snt)
+
     for r in range(NR):
         g.wait_ge(A[r], 4)
         g.remote_dma(blk(T.land, r, h), blk(T.xs, r, h), B[r], T.sem.snt, mate_pid, mate_rid, 255)

@@ -5,7 +5,7 @@ NR = len(WIDTHS)
 STARTS = [4 * sum(WIDTHS[:r]) for r in range(NR)]
 HELP = (2, 3, 6, 7)
 PRE = 2
-LAG = 1
+LAGF = 1.5
 SCRATCH = {'xs': ('sbuf', [128, 16384], 'float32'), 'land': ('sbuf', [128, 16384], 'float32')}
 SEMAPHORES = (['st', 'snt'] + ['l%d' % i for i in range(16)]
               + ['a%d' % i for i in range(16)] + ['b%d' % i for i in range(16)])
@@ -15,7 +15,8 @@ def rank_program(g, core, T, topo):
     A = [T.sem.a0, T.sem.a1, T.sem.a2, T.sem.a3, T.sem.a4, T.sem.a5, T.sem.a6, T.sem.a7, T.sem.a8, T.sem.a9, T.sem.a10, T.sem.a11, T.sem.a12, T.sem.a13, T.sem.a14, T.sem.a15]
     B = [T.sem.b0, T.sem.b1, T.sem.b2, T.sem.b3, T.sem.b4, T.sem.b5, T.sem.b6, T.sem.b7, T.sem.b8, T.sem.b9, T.sem.b10, T.sem.b11, T.sem.b12, T.sem.b13, T.sem.b14, T.sem.b15]
     L = [T.sem.l0, T.sem.l1, T.sem.l2, T.sem.l3, T.sem.l4, T.sem.l5, T.sem.l6, T.sem.l7, T.sem.l8, T.sem.l9, T.sem.l10, T.sem.l11, T.sem.l12, T.sem.l13, T.sem.l14, T.sem.l15]
-    base = topo.chip(core) * 8
+    chip = topo.chip(core)
+    base = chip * 8
     root = base
     on_chip = core - base
 
@@ -50,20 +51,32 @@ def rank_program(g, core, T, topo):
         return
     h = HELP.index(on_chip)
     mate_rid, mate_pid = topo.addr(core ^ 8)[:2]
-    root_rid, root_pid = topo.addr(root)[:2]
+    own_rid, own_pid = topo.addr(root)[:2]
+    oth_rid, oth_pid = topo.addr(root ^ 8)[:2]
 
-    def fold(r):
-        g.wait_ge(B[r], 8)
-        g.remote_dma_fused([bass.RemoteDMATransfer(
-            dst_ids=[bass.DstId(rid=root_rid, pnc=root_pid)], dma_engine_mask=65280,
-            remote_sem=A[r], srcs=[blk(T.xs, r, h), blk(T.land, r, h)],
-            dsts=[blk(T.land, r, h)], alu_op=1)], local_sem=T.sem.snt)
-
+    events = []
     for r in range(NR):
+        if (r + h) % 2 == chip:
+            events.append((r + LAGF, 1, r))
+        else:
+            events.append((float(r), 0, r))
+    events.sort()
+    sent = 0
+    for _, kind, r in events:
         g.wait_ge(A[r], 4)
-        g.remote_dma(blk(T.land, r, h), blk(T.xs, r, h), B[r], T.sem.snt, mate_pid, mate_rid, 255)
-        if r >= LAG:
-            fold(r - LAG)
-    for r in range(NR - LAG, NR):
-        fold(r)
-    g.wait_ge(T.sem.snt, 16 * NR)
+        if kind == 0:
+            g.remote_dma(blk(T.land, r, h), blk(T.xs, r, h), B[r], T.sem.snt, mate_pid, mate_rid, 255)
+            sent += 8
+        else:
+            g.wait_ge(B[r], 8)
+            srcs = [blk(T.xs, r, h), blk(T.land, r, h)]
+            g.remote_dma_fused([
+                bass.RemoteDMATransfer(
+                    dst_ids=[bass.DstId(rid=oth_rid, pnc=oth_pid)], dma_engine_mask=0x00FF,
+                    remote_sem=A[r], srcs=srcs, dsts=[blk(T.land, r, h)], alu_op=1),
+                bass.RemoteDMATransfer(
+                    dst_ids=[bass.DstId(rid=own_rid, pnc=own_pid)], dma_engine_mask=0xFF00,
+                    remote_sem=A[r], srcs=srcs, dsts=[blk(T.land, r, h)], alu_op=1),
+            ], local_sem=T.sem.snt)
+            sent += 16
+    g.wait_ge(T.sem.snt, sent)

@@ -5,7 +5,6 @@ NR = len(WIDTHS)
 STARTS = [4 * sum(WIDTHS[:r]) for r in range(NR)]
 HELP = (2, 3, 6, 7)
 PRE = 2
-LAGF = 1.5
 SCRATCH = {'xs': ('sbuf', [128, 16384], 'float32'), 'land': ('sbuf', [128, 16384], 'float32')}
 SEMAPHORES = (['st', 'snt'] + ['l%d' % i for i in range(16)]
               + ['a%d' % i for i in range(16)] + ['b%d' % i for i in range(16)])
@@ -23,8 +22,12 @@ def rank_program(g, core, T, topo):
     def rnd(t, r):
         return t[:, STARTS[r]:STARTS[r] + 4 * WIDTHS[r]]
 
-    def blk(t, r, h):
-        c = STARTS[r] + h * WIDTHS[r]
+    def blk(t, r, d):
+        c = STARTS[r] + 2 * d * WIDTHS[r]
+        return t[:, c:c + 2 * WIDTHS[r]]
+
+    def half(t, r, d, k):
+        c = STARTS[r] + (2 * d + k) * WIDTHS[r]
         return t[:, c:c + WIDTHS[r]]
 
     if core == root:
@@ -35,11 +38,11 @@ def rank_program(g, core, T, topo):
         for r in range(NR):
             g.wait_ge(L[r], 16)
             trs = []
-            for h in range(4):
-                rid, pid = topo.addr(base + HELP[h])[:2]
+            for d in range(2):
+                rid, pid = topo.addr(base + HELP[2 * d + r % 2])[:2]
                 trs.append(bass.RemoteDMATransfer(
-                    dst_ids=[bass.DstId(rid=rid, pnc=pid)], dma_engine_mask=15 << 4 * h,
-                    remote_sem=A[r], src=blk(T.xs, r, h), dst=blk(T.xs, r, h)))
+                    dst_ids=[bass.DstId(rid=rid, pnc=pid)], dma_engine_mask=255 << 8 * d,
+                    remote_sem=A[r], src=blk(T.xs, r, d), dst=blk(T.xs, r, d)))
             g.remote_dma_fused(trs, local_sem=T.sem.snt)
         for r in range(NR):
             g.scalar.wait_ge(A[r], 32)
@@ -50,33 +53,25 @@ def rank_program(g, core, T, topo):
     if on_chip not in HELP:
         return
     h = HELP.index(on_chip)
+    d = h // 2
     mate_rid, mate_pid = topo.addr(core ^ 8)[:2]
     own_rid, own_pid = topo.addr(root)[:2]
     oth_rid, oth_pid = topo.addr(root ^ 8)[:2]
 
-    events = []
-    for r in range(NR):
-        if (r + h) % 2 == chip:
-            events.append((r + LAGF, 1, r))
-        else:
-            events.append((float(r), 0, r))
-    events.sort()
     sent = 0
-    for _, kind, r in events:
-        g.wait_ge(A[r], 4)
-        if kind == 0:
-            g.remote_dma(blk(T.land, r, h), blk(T.xs, r, h), B[r], T.sem.snt, mate_pid, mate_rid, 255)
-            sent += 8
-        else:
-            g.wait_ge(B[r], 8)
-            srcs = [blk(T.xs, r, h), blk(T.land, r, h)]
-            g.remote_dma_fused([
-                bass.RemoteDMATransfer(
-                    dst_ids=[bass.DstId(rid=oth_rid, pnc=oth_pid)], dma_engine_mask=0x00FF,
-                    remote_sem=A[r], srcs=srcs, dsts=[blk(T.land, r, h)], alu_op=1),
-                bass.RemoteDMATransfer(
-                    dst_ids=[bass.DstId(rid=own_rid, pnc=own_pid)], dma_engine_mask=0xFF00,
-                    remote_sem=A[r], srcs=srcs, dsts=[blk(T.land, r, h)], alu_op=1),
-            ], local_sem=T.sem.snt)
-            sent += 16
+    for r in range(h % 2, NR, 2):
+        g.wait_ge(A[r], 8)
+        g.remote_dma(half(T.land, r, d, 1 - chip), half(T.xs, r, d, 1 - chip), B[r], T.sem.snt,
+                     mate_pid, mate_rid, 255)
+        g.wait_ge(B[r], 8)
+        srcs = [half(T.xs, r, d, chip), half(T.land, r, d, chip)]
+        g.remote_dma_fused([
+            bass.RemoteDMATransfer(
+                dst_ids=[bass.DstId(rid=oth_rid, pnc=oth_pid)], dma_engine_mask=0x00FF,
+                remote_sem=A[r], srcs=srcs, dsts=[half(T.land, r, d, chip)], alu_op=1),
+            bass.RemoteDMATransfer(
+                dst_ids=[bass.DstId(rid=own_rid, pnc=own_pid)], dma_engine_mask=0xFF00,
+                remote_sem=A[r], srcs=srcs, dsts=[half(T.land, r, d, chip)], alu_op=1),
+        ], local_sem=T.sem.snt)
+        sent += 24
     g.wait_ge(T.sem.snt, sent)

@@ -1,6 +1,6 @@
 import concourse.bass as bass
 
-WIDTHS = [128, 384, 512, 512, 512, 512, 512, 512, 384, 128]
+WIDTHS = [128, 128, 256, 512, 512, 512, 512, 512, 512, 384, 128]
 NR = len(WIDTHS)
 STARTS = [4 * sum(WIDTHS[:r]) for r in range(NR)]
 HELP = (2, 3, 6, 7)
@@ -44,6 +44,7 @@ def rank_program(g, core, T, topo):
                     dst_ids=[bass.DstId(rid=rid, pnc=pid)], dma_engine_mask=255 << 8 * d,
                     remote_sem=A[r], src=blk(T.xs, r, d), dst=blk(T.xs, r, d)))
             g.remote_dma_fused(trs, local_sem=T.sem.snt)
+        g.scalar.wait_ge(L[NR - 1], 16)
         for r in range(NR):
             g.scalar.wait_ge(A[r], 32)
             g.scalar.dma_start(rnd(T.y, r), rnd(T.land, r)).then_inc(T.sem.st, 16)

@@ -1,7 +1,8 @@
 import concourse.bass as bass
 
-WIDTHS = [128, 128, 256, 512, 512, 512, 512, 512, 512, 384, 128]
+WIDTHS = [128, 384, 512, 512, 512, 512, 512, 512, 384, 128]
 NR = len(WIDTHS)
+NX = 2
 STARTS = [4 * sum(WIDTHS[:r]) for r in range(NR)]
 HELP = (2, 3, 6, 7)
 PRE = 2
@@ -46,7 +47,7 @@ def rank_program(g, core, T, topo):
             g.remote_dma_fused(trs, local_sem=T.sem.snt)
         g.scalar.wait_ge(L[NR - 1], 16)
         for r in range(NR):
-            g.scalar.wait_ge(A[r], 32)
+            g.scalar.wait_ge(A[r], 16 if r < NX else 32)
             g.scalar.dma_start(rnd(T.y, r), rnd(T.land, r)).then_inc(T.sem.st, 16)
         g.wait_ge(T.sem.snt, 16 * NR)
         g.scalar.wait_ge(T.sem.st, 16 * NR)
@@ -62,6 +63,15 @@ def rank_program(g, core, T, topo):
     sent = 0
     for r in range(h % 2, NR, 2):
         g.wait_ge(A[r], 8)
+        if r < NX:
+            g.remote_dma(blk(T.land, r, d), blk(T.xs, r, d), B[r], T.sem.snt, mate_pid, mate_rid, 255)
+            g.wait_ge(B[r], 8)
+            g.remote_dma_fused([bass.RemoteDMATransfer(
+                dst_ids=[bass.DstId(rid=own_rid, pnc=own_pid)], dma_engine_mask=0xFF00,
+                remote_sem=A[r], srcs=[blk(T.xs, r, d), blk(T.land, r, d)],
+                dsts=[blk(T.land, r, d)], alu_op=1)], local_sem=T.sem.snt)
+            sent += 16
+            continue
         g.remote_dma(half(T.land, r, d, 1 - chip), half(T.xs, r, d, 1 - chip), B[r], T.sem.snt,
                      mate_pid, mate_rid, 255)
         g.wait_ge(B[r], 8)

@@ -3,11 +3,11 @@ import concourse.bass as bass
 WIDTHS = [128, 384, 512, 512, 512, 512, 512, 512, 384, 128]
 NR = len(WIDTHS)
 NX = 2
+GROUPS = [[0, 1, 2], [3, 4], [5], [6], [7], [8], [9]]
 STARTS = [4 * sum(WIDTHS[:r]) for r in range(NR)]
 HELP = (2, 3, 6, 7)
-PRE = 2
 SCRATCH = {'xs': ('sbuf', [128, 16384], 'float32'), 'land': ('sbuf', [128, 16384], 'float32')}
-SEMAPHORES = (['st', 'snt'] + ['l%d' % i for i in range(16)]
+SEMAPHORES = (['st0', 'st1', 'snt'] + ['l%d' % i for i in range(16)] + ['k%d' % i for i in range(10)]
               + ['a%d' % i for i in range(16)] + ['b%d' % i for i in range(16)])
 
 
@@ -15,6 +15,7 @@ def rank_program(g, core, T, topo):
     A = [T.sem.a0, T.sem.a1, T.sem.a2, T.sem.a3, T.sem.a4, T.sem.a5, T.sem.a6, T.sem.a7, T.sem.a8, T.sem.a9, T.sem.a10, T.sem.a11, T.sem.a12, T.sem.a13, T.sem.a14, T.sem.a15]
     B = [T.sem.b0, T.sem.b1, T.sem.b2, T.sem.b3, T.sem.b4, T.sem.b5, T.sem.b6, T.sem.b7, T.sem.b8, T.sem.b9, T.sem.b10, T.sem.b11, T.sem.b12, T.sem.b13, T.sem.b14, T.sem.b15]
     L = [T.sem.l0, T.sem.l1, T.sem.l2, T.sem.l3, T.sem.l4, T.sem.l5, T.sem.l6, T.sem.l7, T.sem.l8, T.sem.l9, T.sem.l10, T.sem.l11, T.sem.l12, T.sem.l13, T.sem.l14, T.sem.l15]
+    K = [T.sem.k0, T.sem.k1, T.sem.k2, T.sem.k3, T.sem.k4, T.sem.k5, T.sem.k6, T.sem.k7, T.sem.k8, T.sem.k9]
     chip = topo.chip(core)
     base = chip * 8
     root = base
@@ -32,10 +33,12 @@ def rank_program(g, core, T, topo):
         return t[:, c:c + WIDTHS[r]]
 
     if core == root:
+        Q = [g.sync, g.scalar]
+        ST = [T.sem.st0, T.sem.st1]
         for r in range(NR):
-            if r >= PRE:
-                g.sync.wait_ge(L[r - PRE], 16)
-            g.sync.dma_start(rnd(T.xs, r), rnd(T.x, r)).then_inc(L[r], 16)
+            if r >= 2:
+                Q[r % 2].wait_ge(K[r - 2], 1)
+            Q[r % 2].dma_start(rnd(T.xs, r), rnd(T.x, r)).then_inc(L[r], 16)
         for r in range(NR):
             g.wait_ge(L[r], 16)
             trs = []
@@ -45,12 +48,22 @@ def rank_program(g, core, T, topo):
                     dst_ids=[bass.DstId(rid=rid, pnc=pid)], dma_engine_mask=255 << 8 * d,
                     remote_sem=A[r], src=blk(T.xs, r, d), dst=blk(T.xs, r, d)))
             g.remote_dma_fused(trs, local_sem=T.sem.snt)
-        g.scalar.wait_ge(L[NR - 1], 16)
-        for r in range(NR):
-            g.scalar.wait_ge(A[r], 16 if r < NX else 32)
-            g.scalar.dma_start(rnd(T.y, r), rnd(T.land, r)).then_inc(T.sem.st, 16)
+            g.sem_inc(K[r], 1)
+        for q in Q:
+            q.wait_ge(K[NR - 2], 1)
+            q.wait_ge(K[NR - 1], 1)
+        n = [0, 0]
+        for i, grp in enumerate(GROUPS):
+            k = i % 2
+            for r in grp:
+                Q[k].wait_ge(A[r], 16 if r < NX else 32)
+            c0 = STARTS[grp[0]]
+            c1 = STARTS[grp[-1]] + 4 * WIDTHS[grp[-1]]
+            Q[k].dma_start(T.y[:, c0:c1], T.land[:, c0:c1]).then_inc(ST[k], 16)
+            n[k] += 16
         g.wait_ge(T.sem.snt, 16 * NR)
-        g.scalar.wait_ge(T.sem.st, 16 * NR)
+        for k in range(2):
+            Q[k].wait_ge(ST[k], n[k])
         return
     if on_chip not in HELP:
         return

import concourse.bass as bass

WIDTHS = [128, 384, 512, 512, 512, 512, 512, 512, 384, 128]
NR = len(WIDTHS)
NX = 2
GROUPS = [[0, 1, 2], [3, 4], [5], [6], [7], [8], [9]]
STARTS = [4 * sum(WIDTHS[:r]) for r in range(NR)]
HELP = (2, 3, 6, 7)
SCRATCH = {'xs': ('sbuf', [128, 16384], 'float32'), 'land': ('sbuf', [128, 16384], 'float32')}
SEMAPHORES = (['st0', 'st1', 'snt'] + ['l%d' % i for i in range(16)] + ['k%d' % i for i in range(10)]
              + ['a%d' % i for i in range(16)] + ['b%d' % i for i in range(16)])


def rank_program(g, core, T, topo):
    A = [T.sem.a0, T.sem.a1, T.sem.a2, T.sem.a3, T.sem.a4, T.sem.a5, T.sem.a6, T.sem.a7, T.sem.a8, T.sem.a9, T.sem.a10, T.sem.a11, T.sem.a12, T.sem.a13, T.sem.a14, T.sem.a15]
    B = [T.sem.b0, T.sem.b1, T.sem.b2, T.sem.b3, T.sem.b4, T.sem.b5, T.sem.b6, T.sem.b7, T.sem.b8, T.sem.b9, T.sem.b10, T.sem.b11, T.sem.b12, T.sem.b13, T.sem.b14, T.sem.b15]
    L = [T.sem.l0, T.sem.l1, T.sem.l2, T.sem.l3, T.sem.l4, T.sem.l5, T.sem.l6, T.sem.l7, T.sem.l8, T.sem.l9, T.sem.l10, T.sem.l11, T.sem.l12, T.sem.l13, T.sem.l14, T.sem.l15]
    K = [T.sem.k0, T.sem.k1, T.sem.k2, T.sem.k3, T.sem.k4, T.sem.k5, T.sem.k6, T.sem.k7, T.sem.k8, T.sem.k9]
    chip = topo.chip(core)
    base = chip * 8
    root = base
    on_chip = core - base

    def rnd(t, r):
        return t[:, STARTS[r]:STARTS[r] + 4 * WIDTHS[r]]

    def blk(t, r, d):
        c = STARTS[r] + 2 * d * WIDTHS[r]
        return t[:, c:c + 2 * WIDTHS[r]]

    def half(t, r, d, k):
        c = STARTS[r] + (2 * d + k) * WIDTHS[r]
        return t[:, c:c + WIDTHS[r]]

    if core == root:
        Q = [g.sync, g.scalar]
        ST = [T.sem.st0, T.sem.st1]
        for r in range(NR):
            if r >= 2:
                Q[r % 2].wait_ge(K[r - 2], 1)
            Q[r % 2].dma_start(rnd(T.xs, r), rnd(T.x, r)).then_inc(L[r], 16)
        for r in range(NR):
            g.wait_ge(L[r], 16)
            trs = []
            for d in range(2):
                rid, pid = topo.addr(base + HELP[2 * d + r % 2])[:2]
                trs.append(bass.RemoteDMATransfer(
                    dst_ids=[bass.DstId(rid=rid, pnc=pid)], dma_engine_mask=255 << 8 * d,
                    remote_sem=A[r], src=blk(T.xs, r, d), dst=blk(T.xs, r, d)))
            g.remote_dma_fused(trs, local_sem=T.sem.snt)
            g.sem_inc(K[r], 1)
        for q in Q:
            q.wait_ge(K[NR - 2], 1)
            q.wait_ge(K[NR - 1], 1)
        n = [0, 0]
        for i, grp in enumerate(GROUPS):
            k = i % 2
            for r in grp:
                Q[k].wait_ge(A[r], 16 if r < NX else 32)
            c0 = STARTS[grp[0]]
            c1 = STARTS[grp[-1]] + 4 * WIDTHS[grp[-1]]
            Q[k].dma_start(T.y[:, c0:c1], T.land[:, c0:c1]).then_inc(ST[k], 16)
            n[k] += 16
        g.wait_ge(T.sem.snt, 16 * NR)
        for k in range(2):
            Q[k].wait_ge(ST[k], n[k])
        return
    if on_chip not in HELP:
        return
    h = HELP.index(on_chip)
    d = h // 2
    mate_rid, mate_pid = topo.addr(core ^ 8)[:2]
    own_rid, own_pid = topo.addr(root)[:2]
    oth_rid, oth_pid = topo.addr(root ^ 8)[:2]

    sent = 0
    for r in range(h % 2, NR, 2):
        g.wait_ge(A[r], 8)
        if r < NX:
            g.remote_dma(blk(T.land, r, d), blk(T.xs, r, d), B[r], T.sem.snt, mate_pid, mate_rid, 255)
            g.wait_ge(B[r], 8)
            g.remote_dma_fused([bass.RemoteDMATransfer(
                dst_ids=[bass.DstId(rid=own_rid, pnc=own_pid)], dma_engine_mask=0xFF00,
                remote_sem=A[r], srcs=[blk(T.xs, r, d), blk(T.land, r, d)],
                dsts=[blk(T.land, r, d)], alu_op=1)], local_sem=T.sem.snt)
            sent += 16
            continue
        g.remote_dma(half(T.land, r, d, 1 - chip), half(T.xs, r, d, 1 - chip), B[r], T.sem.snt,
                     mate_pid, mate_rid, 255)
        g.wait_ge(B[r], 8)
        srcs = [half(T.xs, r, d, chip), half(T.land, r, d, chip)]
        g.remote_dma_fused([
            bass.RemoteDMATransfer(
                dst_ids=[bass.DstId(rid=oth_rid, pnc=oth_pid)], dma_engine_mask=0x00FF,
                remote_sem=A[r], srcs=srcs, dsts=[half(T.land, r, d, chip)], alu_op=1),
            bass.RemoteDMATransfer(
                dst_ids=[bass.DstId(rid=own_rid, pnc=own_pid)], dma_engine_mask=0xFF00,
                remote_sem=A[r], srcs=srcs, dsts=[half(T.land, r, d, chip)], alu_op=1),
        ], local_sem=T.sem.snt)
        sent += 24
    g.wait_ge(T.sem.snt, sent)
